import numpy as np
import ml_dtypes


def mxq(x, axis, fmt="e4m3"):
    dtype, down = {"e4m3": (ml_dtypes.float8_e4m3fn, 7), "e5m2": (ml_dtypes.float8_e5m2, 14)}[fmt]
    v = np.moveaxis(np.asarray(x, np.float32).astype(ml_dtypes.bfloat16).astype(np.float64), axis, -1)
    blocks = v.reshape(v.shape[:-1] + (-1, 32))
    amax = np.abs(blocks).max(-1, keepdims=True)
    byte = np.maximum(np.where(amax > 0, np.frexp(amax)[1] - 1 + 127, 0) - down, 1)
    scale = np.exp2(byte - 127.0)
    codes = (blocks / scale).astype(np.float32).astype(dtype).astype(np.float64)
    return np.moveaxis((codes * scale).reshape(v.shape), -1, axis)


WIDE = False


def mx_kscale(k):
    if not WIDE:
        return np.ones(k)
    levels = np.array([10, -10, 5, -5, 0])
    if k % 512:
        return np.exp2(np.random.permutation(np.resize(levels, k // 32))).repeat(32)
    a = np.empty((k // 512, 16))
    for p in range(k // 512):
        a[p, :8] = np.random.permutation(np.resize(levels, 8))
        for g in range(8):
            far = levels[np.abs(levels - a[p, g]) >= 10]
            a[p, g + 8] = far[np.random.randint(len(far))]
    return np.exp2(a.ravel()).repeat(32)


def f64(x):
    return np.asarray(x).astype(np.float64)


def striped(idx):
    return np.tile(idx.reshape(-1, 16).T, (8, 1)).astype(np.uint16)


def unstriped(offs):
    return offs[:16].T.reshape(-1).astype(np.int64)


def silu(v):
    return v / (1.0 + np.exp(-np.maximum(v, -700.0)))


K, T, S, J, H, N = 512, 4096, 1024, 512, 512, 128


def setup_inputs():
    n = np.random.standard_normal
    s = mx_kscale(K)[:, None]
    u = mx_kscale(H)
    r = mx_kscale(J)[:, None]
    return {
        "xT": (n((K, T)) * s).astype(np.float32),
        "eT": (n((J, S)) * r).astype(np.float32),
        "w1": (n((K, H)) / np.sqrt(K) / s * u).astype(np.float32),
        "w3": (n((J, H)) / np.sqrt(J) / r).astype(np.float32),
        "w2": (n((H, N)) / np.sqrt(H) / u[:, None]).astype(np.float32),
        "offs": striped(np.random.permutation(T)[:S]),
    }


def reference(xT, eT, w1, w3, w2, offs):
    c = mxq(f64(w1), 0, "e4m3").T @ mxq(f64(xT)[:, unstriped(offs)], 0, "e4m3")
    z = c * silu(mxq(f64(w3), 0, "e4m3").T @ mxq(f64(eT), 0, "e4m3"))
    return mxq(f64(w2), 0, "e4m3").T @ mxq(z, 0, "e4m3")

@@ -1,0 +1,232 @@
+from contextlib import ExitStack
+
+import concourse.mybir as mybir
+
+F32 = mybir.dt.float32
+BF16 = mybir.dt.bfloat16
+U32 = mybir.dt.uint32
+U16 = mybir.dt.uint16
+U8 = mybir.dt.uint8
+FP8X4 = mybir.dt.float8_e4m3fn_x4
+SILU = mybir.ActivationFunctionType.Silu
+MULT = mybir.AluOpType.mult
+ADD = mybir.AluOpType.add
+
+P = 128
+T, S, H, N = 4096, 1024, 512, 128
+FLOPS = 2 * 512 * H * S * 2 + 2 * H * N * S
+HALF = 512
+CH = 256
+U = 128
+
+
+def tile_picked_schnet_silu_e_kernel(tc, xT, eT, w1, w3, w2, offs, out):
+    nc = tc.nc
+    with ExitStack() as ctx:
+        keep = ctx.enter_context(tc.tile_pool(name="keep", bufs=1))
+        ring = ctx.enter_context(tc.tile_pool(name="ring", bufs=3))
+        psum = ctx.enter_context(tc.psum_pool(name="psum", bufs=3))
+
+        offsets = keep.tile([P, S // 16], U16, name="offsets")
+        x_rows = xT.rearrange("(p t) n -> p t n", t=4)
+        e_rows = eT.rearrange("(p j) n -> p j n", j=4)
+        planes = [keep.tile([P, T], F32, name=f"plane{t}") for t in range(4)]
+        raw = {}
+        raw["w1"] = keep.tile([P, 4, H], F32, name="w1_raw")
+        raw["w3"] = keep.tile([P, 4, H], F32, name="w3_raw")
+        raw["w2"] = keep.tile([P, 4, N], F32, name="w2_raw")
+        e_raw = [keep.tile([P, 4, CH], F32, name=f"e_raw{k}") for k in range(S // CH)]
+
+        nc.sync.dma_start(offsets[:], offs)
+        for what in ["x0","x1","x2","x3","w3","w1","e0","e1","w2","e2","e3"]:
+            if what[0] == "x":
+                t = int(what[1])
+                nc.sync.dma_start(out=planes[t][:], in_=x_rows[:, t, :])
+            elif what == "w1":
+                nc.sync.dma_start(out=raw["w1"][:], in_=w1.rearrange("(p j) c -> p j c", j=4))
+            elif what == "w3":
+                nc.sync.dma_start(out=raw["w3"][:], in_=w3.rearrange("(p j) c -> p j c", j=4))
+            elif what == "w2":
+                nc.sync.dma_start(out=raw["w2"][:], in_=w2.rearrange("(p j) c -> p j c", j=4))
+            else:
+                k = int(what[1])
+                nc.sync.dma_start(out=e_raw[k][:], in_=e_rows[:, :, k * CH : (k + 1) * CH])
+
+        warm = keep.tile([P, 1], F32, name="warm")
+        nc.vector.memset(warm[:], 0.0)
+        nc.scalar.activation(out=warm[:], in_=warm[:], func=SILU)
+
+        def copy_on(engine, dst, src):
+            if engine == "S":
+                nc.scalar.copy(out=dst, in_=src)
+            elif engine == "V":
+                nc.vector.tensor_copy(out=dst, in_=src)
+            else:
+                nc.gpsimd.tensor_scalar(out=dst, in0=src, scalar1=1.0, scalar2=0.0, op0=MULT, op1=ADD)
+
+        codes = {}
+        scales = {}
+        grouped = {}
+
+        def interleave_w(name, engine):
+            width = raw[name].shape[2]
+            g = keep.tile([P, width * 4], BF16, align_bytes=64, name=f"{name}_grouped")
+            grouped[name] = g
+            if name == "w2":
+                copy_on(engine, g[:].rearrange("p (n j) -> p n j", j=4), raw[name][:].rearrange("p j n -> p n j"))
+            else:
+                copy_on(
+                    engine,
+                    g[:].rearrange("p (t m j) -> p m t j", t=4, j=4),
+                    raw[name][:].rearrange("p j (m t) -> p m t j", t=4),
+                )
+
+        def quantize(name, width):
+            c = keep.tile([P, width], U32, align_bytes=64, name=f"{name}_codes")
+            s = keep.tile([P, width], U8, align_bytes=64, name=f"{name}_scales")
+            codes[name] = c
+            scales[name] = s
+            nc.vector.quantize_mx(out=c[:].bitcast(FP8X4), scales=s[:], in_=grouped[name][:])
+
+        def interleave_e(k, engine):
+            g = keep.tile([P, CH * 4], BF16, align_bytes=64, name=f"e{k}_grouped")
+            grouped[f"e{k}"] = g
+            copy_on(
+                engine,
+                g[:].rearrange("p (c i j) -> p c j i", i=4, j=4),
+                e_raw[k][:].rearrange("p j (c i) -> p c j i", i=4),
+            )
+
+        x_grouped = [keep.tile([P, HALF, 4], BF16, align_bytes=64, name=f"x{h}_grouped") for h in range(2)]
+
+        def gather(t, h):
+            nc.vector.tensor_copy(
+                x_grouped[h][:, :, t], planes[t][:].indirect(offsets[:, h * HALF // 16 : (h + 1) * HALF // 16])
+            )
+
+        def quantize_x(h):
+            c = keep.tile([P, HALF], U32, align_bytes=64, name=f"x{h}_codes")
+            s = keep.tile([P, HALF], U8, align_bytes=64, name=f"x{h}_scales")
+            codes[f"x{h}"] = c
+            scales[f"x{h}"] = s
+            nc.vector.quantize_mx(
+                out=c[:].bitcast(FP8X4), scales=s[:], in_=x_grouped[h][:].rearrange("p n j -> p (n j)")
+            )
+
+        def product(w, x, c0, acc):
+            for t in range(4):
+                nc.tensor.matmul_mx(
+                    out=acc[:, t, :],
+                    lhsT=codes[w][:, t * P : (t + 1) * P].bitcast(FP8X4),
+                    lhsT_scale=scales[w][:, t * P : (t + 1) * P],
+                    rhs=codes[x][:, c0 : c0 + U].bitcast(FP8X4),
+                    rhs_scale=scales[x][:, c0 : c0 + U],
+                    start=True,
+                    stop=True,
+                )
+
+        filt = {}
+        cacc = {}
+        z_tiles = {}
+
+        def f_unit(u):
+            acc = psum.tile([P, 4, U], F32, name="f_acc")
+            product("w3", f"e{u * U // CH}", u * U % CH, acc)
+            s = ring.tile([P, U, 4], F32, name="filter", bufs=4)
+            filt[u] = s
+            nc.scalar.activation(out=s[:], in_=acc[:].rearrange("p t n -> p n t"), func=SILU)
+
+        def c_unit(u):
+            acc = psum.tile([P, 4, U], F32, name="c_acc")
+            cacc[u] = acc
+            product("w1", f"x{u * U // HALF}", u * U % HALF, acc)
+
+        def mult(u, z, col):
+            nc.vector.tensor_tensor(
+                out=z[:, col * 4 : (col + U) * 4].rearrange("p (n t) -> p n t", t=4),
+                in0=cacc[u][:].rearrange("p t n -> p n t"),
+                in1=filt[u][:],
+                op=MULT,
+            )
+
+        def new_z(g):
+            n = len(g) * U
+            z_tiles[g[0]] = keep.tile([P, n * 4], BF16, align_bytes=64, name=f"z{g[0]}")
+
+        def finish(g, engine):
+            n = len(g) * U
+            zc = keep.tile([P, n], U32, align_bytes=64, name=f"z{g[0]}_codes")
+            zs = keep.tile([P, n], U8, align_bytes=64, name=f"z{g[0]}_scales")
+            nc.vector.quantize_mx(out=zc[:].bitcast(FP8X4), scales=zs[:], in_=z_tiles[g[0]][:])
+            acc = psum.tile([P, n], F32, name="o_acc", bufs=2)
+            nc.tensor.matmul_mx(
+                out=acc[:],
+                lhsT=codes["w2"][:].bitcast(FP8X4),
+                lhsT_scale=scales["w2"][:],
+                rhs=zc[:].bitcast(FP8X4),
+                rhs_scale=zs[:],
+                start=True,
+                stop=True,
+            )
+            y = keep.tile([P, n], F32, name=f"y{g[0]}")
+            copy_on(engine, y[:], acc[:])
+            nc.sync.dma_start(out=out[:, g[0] * U : g[0] * U + n], in_=y[:])
+
+        gather(0, 0)
+        gather(0, 1)
+        gather(1, 0)
+        gather(1, 1)
+        gather(2, 0)
+        gather(2, 1)
+        gather(3, 0)
+        gather(3, 1)
+        quantize_x(0)
+        quantize_x(1)
+        interleave_w("w3", "S")
+        quantize("w3", 512)
+        interleave_e(0, "V")
+        quantize("e0", CH)
+        interleave_w("w1", "G")
+        quantize("w1", 512)
+        f_unit(0)
+        f_unit(1)
+        c_unit(0)
+        c_unit(1)
+        interleave_e(1, "S")
+        quantize("e1", CH)
+        interleave_w("w2", "G")
+        quantize("w2", 128)
+        f_unit(2)
+        f_unit(3)
+        new_z([0,1])
+        mult(0, z_tiles[0], (0 - 0) * U)
+        mult(1, z_tiles[0], (1 - 0) * U)
+        interleave_e(2, "G")
+        quantize("e2", CH)
+        c_unit(2)
+        c_unit(3)
+        finish([0,1], "S")
+        f_unit(4)
+        f_unit(5)
+        new_z([2,3])
+        mult(2, z_tiles[2], (2 - 2) * U)
+        mult(3, z_tiles[2], (3 - 2) * U)
+        interleave_e(3, "G")
+        quantize("e3", CH)
+        c_unit(4)
+        c_unit(5)
+        finish([2,3], "S")
+        f_unit(6)
+        f_unit(7)
+        new_z([4,5])
+        mult(4, z_tiles[4], (4 - 4) * U)
+        mult(5, z_tiles[4], (5 - 4) * U)
+        c_unit(6)
+        c_unit(7)
+        finish([4,5], "S")
+        new_z([6])
+        mult(6, z_tiles[6], (6 - 6) * U)
+        new_z([7])
+        mult(7, z_tiles[7], (7 - 7) * U)
+        finish([6], "S")
+        finish([7], "S")

@@ -38,7 +38,7 @@ def tile_picked_schnet_silu_e_kernel(tc, xT, eT, w1, w3, w2, offs, out):
         e_raw = [keep.tile([P, 4, CH], F32, name=f"e_raw{k}") for k in range(S // CH)]
 
         nc.sync.dma_start(offsets[:], offs)
-        for what in ["x0","x1","x2","x3","w3","w1","e0","e1","w2","e2","e3"]:
+        for what in ["x0","x1","x2","x3","w1","w3","e0","e1","e2","w2","e3"]:
             if what[0] == "x":
                 t = int(what[1])
                 nc.sync.dma_start(out=planes[t][:], in_=x_rows[:, t, :])
@@ -68,18 +68,23 @@ def tile_picked_schnet_silu_e_kernel(tc, xT, eT, w1, w3, w2, offs, out):
         scales = {}
         grouped = {}
 
-        def interleave_w(name, engine):
-            width = raw[name].shape[2]
-            g = keep.tile([P, width * 4], BF16, align_bytes=64, name=f"{name}_grouped")
-            grouped[name] = g
-            if name == "w2":
-                copy_on(engine, g[:].rearrange("p (n j) -> p n j", j=4), raw[name][:].rearrange("p j n -> p n j"))
-            else:
-                copy_on(
-                    engine,
-                    g[:].rearrange("p (t m j) -> p m t j", t=4, j=4),
-                    raw[name][:].rearrange("p j (m t) -> p m t j", t=4),
-                )
+        def new_w(name):
+            grouped[name] = keep.tile([P, raw[name].shape[2] * 4], BF16, align_bytes=64, name=f"{name}_grouped")
+
+        def interleave_w2(engine):
+            new_w("w2")
+            copy_on(
+                engine,
+                grouped["w2"][:].rearrange("p (c i j) -> p c j i", i=4, j=4),
+                raw["w2"][:].rearrange("p j (c i) -> p c j i", i=4),
+            )
+
+        def interleave_w(name, engine, t0, t1):
+            copy_on(
+                engine,
+                grouped[name][:].rearrange("p (t m j) -> p m t j", t=4, j=4)[:, :, t0:t1, :],
+                raw[name][:].rearrange("p j (m t) -> p m t j", t=4)[:, :, t0:t1, :],
+            )
 
         def quantize(name, width):
             c = keep.tile([P, width], U32, align_bytes=64, name=f"{name}_codes")
@@ -149,6 +154,13 @@ def tile_picked_schnet_silu_e_kernel(tc, xT, eT, w1, w3, w2, offs, out):
                 op=MULT,
             )
 
+        def mult_g(u, z, col):
+            cs = ring.tile([P, U, 4], F32, name="c_sbuf", bufs=2)
+            nc.scalar.copy(out=cs[:], in_=cacc[u][:].rearrange("p t n -> p n t"))
+            nc.gpsimd.tensor_tensor(
+                out=z[:, col * 4 : (col + U) * 4].rearrange("p (n t) -> p n t", t=4), in0=cs[:], in1=filt[u][:], op=MULT
+            )
+
         def new_z(g):
             n = len(g) * U
             z_tiles[g[0]] = keep.tile([P, n * 4], BF16, align_bytes=64, name=f"z{g[0]}")
@@ -182,45 +194,49 @@ def tile_picked_schnet_silu_e_kernel(tc, xT, eT, w1, w3, w2, offs, out):
         gather(3, 1)
         quantize_x(0)
         quantize_x(1)
-        interleave_w("w3", "S")
+        new_w("w1")
+        interleave_w("w1", "S", 0, 2)
+        interleave_w("w1", "S", 2, 4)
+        quantize("w1", 512)
+        c_unit(0)
+        c_unit(1)
+        c_unit(2)
+        new_w("w3")
+        interleave_w("w3", "S", 0, 2)
+        interleave_w("w3", "G", 2, 4)
         quantize("w3", 512)
         interleave_e(0, "V")
         quantize("e0", CH)
-        interleave_w("w1", "G")
-        quantize("w1", 512)
         f_unit(0)
         f_unit(1)
-        c_unit(0)
-        c_unit(1)
         interleave_e(1, "S")
         quantize("e1", CH)
-        interleave_w("w2", "G")
-        quantize("w2", 128)
+        interleave_e(2, "V")
+        quantize("e2", CH)
         f_unit(2)
         f_unit(3)
+        interleave_w2("G")
+        quantize("w2", 128)
         new_z([0,1])
         mult(0, z_tiles[0], (0 - 0) * U)
-        mult(1, z_tiles[0], (1 - 0) * U)
-        interleave_e(2, "G")
-        quantize("e2", CH)
-        c_unit(2)
+        mult_g(1, z_tiles[0], (1 - 0) * U)
+        interleave_e(3, "V")
+        quantize("e3", CH)
         c_unit(3)
-        finish([0,1], "S")
         f_unit(4)
         f_unit(5)
         new_z([2,3])
         mult(2, z_tiles[2], (2 - 2) * U)
-        mult(3, z_tiles[2], (3 - 2) * U)
-        interleave_e(3, "G")
-        quantize("e3", CH)
+        mult_g(3, z_tiles[2], (3 - 2) * U)
+        finish([0,1], "S")
         c_unit(4)
         c_unit(5)
-        finish([2,3], "S")
         f_unit(6)
         f_unit(7)
         new_z([4,5])
         mult(4, z_tiles[4], (4 - 4) * U)
         mult(5, z_tiles[4], (5 - 4) * U)
+        finish([2,3], "S")
         c_unit(6)
         c_unit(7)
         finish([4,5], "S")

@@ -38,7 +38,7 @@ def tile_picked_schnet_silu_e_kernel(tc, xT, eT, w1, w3, w2, offs, out):
         e_raw = [keep.tile([P, 4, CH], F32, name=f"e_raw{k}") for k in range(S // CH)]
 
         nc.sync.dma_start(offsets[:], offs)
-        for what in ["x0","x1","x2","x3","w1","w3","e0","e1","e2","w2","e3"]:
+        for what in ["x0","x1","x2","x3","w1","w3","e0","e1","e2","e3","w2"]:
             if what[0] == "x":
                 t = int(what[1])
                 nc.sync.dma_start(out=planes[t][:], in_=x_rows[:, t, :])
@@ -104,10 +104,17 @@ def tile_picked_schnet_silu_e_kernel(tc, xT, eT, w1, w3, w2, offs, out):
 
         x_grouped = [keep.tile([P, HALF, 4], BF16, align_bytes=64, name=f"x{h}_grouped") for h in range(2)]
 
+        x_pair = [keep.tile([P, 2, HALF], F32, name=f"x{h}_pair") for h in range(2)]
+
         def gather(t, h):
-            nc.vector.tensor_copy(
-                x_grouped[h][:, :, t], planes[t][:].indirect(offsets[:, h * HALF // 16 : (h + 1) * HALF // 16])
-            )
+            picked = planes[t][:].indirect(offsets[:, h * HALF // 16 : (h + 1) * HALF // 16])
+            if t < 2:
+                nc.vector.tensor_copy(x_grouped[h][:, :, t], picked)
+            else:
+                nc.vector.tensor_copy(x_pair[h][:, t - 2, :], picked)
+
+        def pair(h):
+            nc.scalar.copy(out=x_grouped[h][:, :, 2:4], in_=x_pair[h][:].rearrange("p u n -> p n u"))
 
         def quantize_x(h):
             c = keep.tile([P, HALF], U32, align_bytes=64, name=f"x{h}_codes")
@@ -132,14 +139,20 @@ def tile_picked_schnet_silu_e_kernel(tc, xT, eT, w1, w3, w2, offs, out):
 
         filt = {}
         cacc = {}
+        facc = {}
+        oacc = {}
+        zc_tiles = {}
         z_tiles = {}
 
         def f_unit(u):
             acc = psum.tile([P, 4, U], F32, name="f_acc")
             product("w3", f"e{u * U // CH}", u * U % CH, acc)
-            s = ring.tile([P, U, 4], F32, name="filter", bufs=4)
+            facc[u] = acc
+
+        def silu(u):
+            s = ring.tile([P, U, 4], F32, name="filter", bufs=8)
             filt[u] = s
-            nc.scalar.activation(out=s[:], in_=acc[:].rearrange("p t n -> p n t"), func=SILU)
+            nc.scalar.activation(out=s[:], in_=facc[u][:].rearrange("p t n -> p n t"), func=SILU)
 
         def c_unit(u):
             acc = psum.tile([P, 4, U], F32, name="c_acc")
@@ -155,7 +168,7 @@ def tile_picked_schnet_silu_e_kernel(tc, xT, eT, w1, w3, w2, offs, out):
             )
 
         def mult_g(u, z, col):
-            cs = ring.tile([P, U, 4], F32, name="c_sbuf", bufs=2)
+            cs = ring.tile([P, U, 4], F32, name="c_sbuf", bufs=4)
             nc.scalar.copy(out=cs[:], in_=cacc[u][:].rearrange("p t n -> p n t"))
             nc.gpsimd.tensor_tensor(
                 out=z[:, col * 4 : (col + U) * 4].rearrange("p (n t) -> p n t", t=4), in0=cs[:], in1=filt[u][:], op=MULT
@@ -165,12 +178,17 @@ def tile_picked_schnet_silu_e_kernel(tc, xT, eT, w1, w3, w2, offs, out):
             n = len(g) * U
             z_tiles[g[0]] = keep.tile([P, n * 4], BF16, align_bytes=64, name=f"z{g[0]}")
 
-        def finish(g, engine):
+        def quantize_z(g):
             n = len(g) * U
             zc = keep.tile([P, n], U32, align_bytes=64, name=f"z{g[0]}_codes")
             zs = keep.tile([P, n], U8, align_bytes=64, name=f"z{g[0]}_scales")
             nc.vector.quantize_mx(out=zc[:].bitcast(FP8X4), scales=zs[:], in_=z_tiles[g[0]][:])
-            acc = psum.tile([P, n], F32, name="o_acc", bufs=2)
+            zc_tiles[g[0]] = (zc, zs)
+
+        def project(g):
+            zc, zs = zc_tiles[g[0]]
+            acc = psum.tile([P, len(g) * U], F32, name="o_acc", bufs=2)
+            oacc[g[0]] = acc
             nc.tensor.matmul_mx(
                 out=acc[:],
                 lhsT=codes["w2"][:].bitcast(FP8X4),
@@ -180,6 +198,10 @@ def tile_picked_schnet_silu_e_kernel(tc, xT, eT, w1, w3, w2, offs, out):
                 start=True,
                 stop=True,
             )
+
+        def store(g, engine):
+            n = len(g) * U
+            acc = oacc[g[0]]
             y = keep.tile([P, n], F32, name=f"y{g[0]}")
             copy_on(engine, y[:], acc[:])
             nc.sync.dma_start(out=out[:, g[0] * U : g[0] * U + n], in_=y[:])
@@ -192,57 +214,77 @@ def tile_picked_schnet_silu_e_kernel(tc, xT, eT, w1, w3, w2, offs, out):
         gather(2, 1)
         gather(3, 0)
         gather(3, 1)
+        pair(0)
+        new_w("w1")
+        interleave_w("w1", "V", 2, 4)
+        pair(1)
+        interleave_w("w1", "V", 0, 2)
         quantize_x(0)
         quantize_x(1)
-        new_w("w1")
-        interleave_w("w1", "S", 0, 2)
-        interleave_w("w1", "S", 2, 4)
-        quantize("w1", 512)
-        c_unit(0)
-        c_unit(1)
-        c_unit(2)
         new_w("w3")
+        interleave_w("w3", "S", 2, 4)
+        quantize("w1", 512)
         interleave_w("w3", "S", 0, 2)
-        interleave_w("w3", "G", 2, 4)
-        quantize("w3", 512)
+        c_unit(1)
         interleave_e(0, "V")
+        c_unit(0)
         quantize("e0", CH)
+        c_unit(2)
+        quantize("w3", 512)
+        interleave_e(1, "S")
         f_unit(0)
         f_unit(1)
-        interleave_e(1, "S")
+        silu(0)
         quantize("e1", CH)
         interleave_e(2, "V")
-        quantize("e2", CH)
         f_unit(2)
+        silu(1)
         f_unit(3)
-        interleave_w2("G")
-        quantize("w2", 128)
-        new_z([0,1])
-        mult(0, z_tiles[0], (0 - 0) * U)
-        mult_g(1, z_tiles[0], (1 - 0) * U)
-        interleave_e(3, "V")
-        quantize("e3", CH)
+        new_z([0, 1])
+        mult(0, z_tiles[0], 0 * U)
+        silu(2)
+        quantize("e2", CH)
         c_unit(3)
+        interleave_e(3, "S")
+        new_z([2, 3])
+        mult(2, z_tiles[2], 0 * U)
         f_unit(4)
         f_unit(5)
-        new_z([2,3])
-        mult(2, z_tiles[2], (2 - 2) * U)
-        mult_g(3, z_tiles[2], (3 - 2) * U)
-        finish([0,1], "S")
-        c_unit(4)
+        mult(1, z_tiles[0], 1 * U)
+        silu(3)
         c_unit(5)
+        quantize("e3", CH)
+        c_unit(4)
+        silu(5)
+        quantize_z([0, 1])
         f_unit(6)
-        f_unit(7)
-        new_z([4,5])
-        mult(4, z_tiles[4], (4 - 4) * U)
-        mult(5, z_tiles[4], (5 - 4) * U)
-        finish([2,3], "S")
+        mult(3, z_tiles[2], 1 * U)
+        interleave_w2("S")
+        new_z([4, 5])
+        mult(5, z_tiles[4], 1 * U)
         c_unit(6)
-        c_unit(7)
-        finish([4,5], "S")
+        silu(4)
+        quantize("w2", 128)
+        quantize_z([2, 3])
+        silu(6)
+        project([0, 1])
+        f_unit(7)
+        mult(4, z_tiles[4], 0 * U)
+        store([0, 1], "S")
+        project([2, 3])
+        silu(7)
         new_z([6])
-        mult(6, z_tiles[6], (6 - 6) * U)
+        mult(6, z_tiles[6], 0 * U)
+        c_unit(7)
+        store([2, 3], "S")
+        quantize_z([4, 5])
         new_z([7])
-        mult(7, z_tiles[7], (7 - 7) * U)
-        finish([6], "S")
-        finish([7], "S")
+        mult(7, z_tiles[7], 0 * U)
+        project([4, 5])
+        store([4, 5], "S")
+        quantize_z([6])
+        quantize_z([7])
+        project([6])
+        store([6], "S")
+        project([7])
+        store([7], "S")

@@ -37,11 +37,12 @@ def tile_picked_schnet_silu_e_kernel(tc, xT, eT, w1, w3, w2, offs, out):
         raw["w2"] = keep.tile([P, 4, N], F32, name="w2_raw")
         e_raw = [keep.tile([P, 4, CH], F32, name=f"e_raw{k}") for k in range(S // CH)]
 
-        nc.sync.dma_start(offsets[:], offs)
-        for what in ["x0","x1","x2","x3","w1","w3","e0","e1","e2","e3","w2"]:
+        for what in ["x0","x1","x2","x3","w1","w3","e0","e1","e2","w2","e3"]:
             if what[0] == "x":
                 t = int(what[1])
                 nc.sync.dma_start(out=planes[t][:], in_=x_rows[:, t, :])
+                if t == 0:
+                    nc.sync.dma_start(offsets[:], offs)
             elif what == "w1":
                 nc.sync.dma_start(out=raw["w1"][:], in_=w1.rearrange("(p j) c -> p j c", j=4))
             elif what == "w3":
@@ -104,17 +105,10 @@ def tile_picked_schnet_silu_e_kernel(tc, xT, eT, w1, w3, w2, offs, out):
 
         x_grouped = [keep.tile([P, HALF, 4], BF16, align_bytes=64, name=f"x{h}_grouped") for h in range(2)]
 
-        x_pair = [keep.tile([P, 2, HALF], F32, name=f"x{h}_pair") for h in range(2)]
-
         def gather(t, h):
-            picked = planes[t][:].indirect(offsets[:, h * HALF // 16 : (h + 1) * HALF // 16])
-            if t < 2:
-                nc.vector.tensor_copy(x_grouped[h][:, :, t], picked)
-            else:
-                nc.vector.tensor_copy(x_pair[h][:, t - 2, :], picked)
-
-        def pair(h):
-            nc.scalar.copy(out=x_grouped[h][:, :, 2:4], in_=x_pair[h][:].rearrange("p u n -> p n u"))
+            nc.vector.tensor_copy(
+                x_grouped[h][:, :, t], planes[t][:].indirect(offsets[:, h * HALF // 16 : (h + 1) * HALF // 16])
+            )
 
         def quantize_x(h):
             c = keep.tile([P, HALF], U32, align_bytes=64, name=f"x{h}_codes")
@@ -214,22 +208,20 @@ def tile_picked_schnet_silu_e_kernel(tc, xT, eT, w1, w3, w2, offs, out):
         gather(2, 1)
         gather(3, 0)
         gather(3, 1)
-        pair(0)
         new_w("w1")
-        interleave_w("w1", "V", 2, 4)
-        pair(1)
-        interleave_w("w1", "V", 0, 2)
+        interleave_w("w1", "G", 2, 4)
+        interleave_w("w1", "S", 0, 2)
         quantize_x(0)
         quantize_x(1)
-        new_w("w3")
-        interleave_w("w3", "S", 2, 4)
         quantize("w1", 512)
+        new_w("w3")
         interleave_w("w3", "S", 0, 2)
-        c_unit(1)
-        interleave_e(0, "V")
         c_unit(0)
-        quantize("e0", CH)
+        c_unit(1)
         c_unit(2)
+        interleave_w("w3", "S", 2, 4)
+        interleave_e(0, "V")
+        quantize("e0", CH)
         quantize("w3", 512)
         interleave_e(1, "S")
         f_unit(0)
@@ -239,44 +231,44 @@ def tile_picked_schnet_silu_e_kernel(tc, xT, eT, w1, w3, w2, offs, out):
         interleave_e(2, "V")
         f_unit(2)
         silu(1)
+        interleave_w2("G")
         f_unit(3)
         new_z([0, 1])
         mult(0, z_tiles[0], 0 * U)
         silu(2)
         quantize("e2", CH)
+        silu(3)
         c_unit(3)
+        mult(1, z_tiles[0], 1 * U)
+        f_unit(4)
         interleave_e(3, "S")
+        f_unit(5)
+        quantize("w2", 128)
+        quantize_z([0, 1])
+        c_unit(4)
         new_z([2, 3])
         mult(2, z_tiles[2], 0 * U)
-        f_unit(4)
-        f_unit(5)
-        mult(1, z_tiles[0], 1 * U)
-        silu(3)
-        c_unit(5)
-        quantize("e3", CH)
-        c_unit(4)
-        silu(5)
-        quantize_z([0, 1])
-        f_unit(6)
-        mult(3, z_tiles[2], 1 * U)
-        interleave_w2("S")
-        new_z([4, 5])
-        mult(5, z_tiles[4], 1 * U)
-        c_unit(6)
-        silu(4)
-        quantize("w2", 128)
-        quantize_z([2, 3])
-        silu(6)
         project([0, 1])
-        f_unit(7)
-        mult(4, z_tiles[4], 0 * U)
+        silu(4)
+        quantize("e3", CH)
+        c_unit(5)
         store([0, 1], "S")
-        project([2, 3])
+        mult(3, z_tiles[2], 1 * U)
+        f_unit(6)
+        silu(5)
+        f_unit(7)
+        new_z([4, 5])
+        mult(4, z_tiles[4], 0 * U)
+        silu(6)
+        c_unit(6)
+        quantize_z([2, 3])
+        c_unit(7)
         silu(7)
+        mult(5, z_tiles[4], 1 * U)
+        project([2, 3])
+        store([2, 3], "S")
         new_z([6])
         mult(6, z_tiles[6], 0 * U)
-        c_unit(7)
-        store([2, 3], "S")
         quantize_z([4, 5])
         new_z([7])
         mult(7, z_tiles[7], 0 * U)

from contextlib import ExitStack

import concourse.mybir as mybir

F32 = mybir.dt.float32
BF16 = mybir.dt.bfloat16
U32 = mybir.dt.uint32
U16 = mybir.dt.uint16
U8 = mybir.dt.uint8
FP8X4 = mybir.dt.float8_e4m3fn_x4
SILU = mybir.ActivationFunctionType.Silu
MULT = mybir.AluOpType.mult
ADD = mybir.AluOpType.add

P = 128
T, S, H, N = 4096, 1024, 512, 128
FLOPS = 2 * 512 * H * S * 2 + 2 * H * N * S
HALF = 512
CH = 256
U = 128


def tile_picked_schnet_silu_e_kernel(tc, xT, eT, w1, w3, w2, offs, out):
    nc = tc.nc
    with ExitStack() as ctx:
        keep = ctx.enter_context(tc.tile_pool(name="keep", bufs=1))
        ring = ctx.enter_context(tc.tile_pool(name="ring", bufs=3))
        psum = ctx.enter_context(tc.psum_pool(name="psum", bufs=3))

        offsets = keep.tile([P, S // 16], U16, name="offsets")
        x_rows = xT.rearrange("(p t) n -> p t n", t=4)
        e_rows = eT.rearrange("(p j) n -> p j n", j=4)
        planes = [keep.tile([P, T], F32, name=f"plane{t}") for t in range(4)]
        raw = {}
        raw["w1"] = keep.tile([P, 4, H], F32, name="w1_raw")
        raw["w3"] = keep.tile([P, 4, H], F32, name="w3_raw")
        raw["w2"] = keep.tile([P, 4, N], F32, name="w2_raw")
        e_raw = [keep.tile([P, 4, CH], F32, name=f"e_raw{k}") for k in range(S // CH)]

        for what in ["x0","x1","x2","x3","w1","w3","e0","e1","e2","w2","e3"]:
            if what[0] == "x":
                t = int(what[1])
                nc.sync.dma_start(out=planes[t][:], in_=x_rows[:, t, :])
                if t == 0:
                    nc.sync.dma_start(offsets[:], offs)
            elif what == "w1":
                nc.sync.dma_start(out=raw["w1"][:], in_=w1.rearrange("(p j) c -> p j c", j=4))
            elif what == "w3":
                nc.sync.dma_start(out=raw["w3"][:], in_=w3.rearrange("(p j) c -> p j c", j=4))
            elif what == "w2":
                nc.sync.dma_start(out=raw["w2"][:], in_=w2.rearrange("(p j) c -> p j c", j=4))
            else:
                k = int(what[1])
                nc.sync.dma_start(out=e_raw[k][:], in_=e_rows[:, :, k * CH : (k + 1) * CH])

        warm = keep.tile([P, 1], F32, name="warm")
        nc.vector.memset(warm[:], 0.0)
        nc.scalar.activation(out=warm[:], in_=warm[:], func=SILU)

        def copy_on(engine, dst, src):
            if engine == "S":
                nc.scalar.copy(out=dst, in_=src)
            elif engine == "V":
                nc.vector.tensor_copy(out=dst, in_=src)
            else:
                nc.gpsimd.tensor_scalar(out=dst, in0=src, scalar1=1.0, scalar2=0.0, op0=MULT, op1=ADD)

        codes = {}
        scales = {}
        grouped = {}

        def new_w(name):
            grouped[name] = keep.tile([P, raw[name].shape[2] * 4], BF16, align_bytes=64, name=f"{name}_grouped")

        def interleave_w2(engine):
            new_w("w2")
            copy_on(
                engine,
                grouped["w2"][:].rearrange("p (c i j) -> p c j i", i=4, j=4),
                raw["w2"][:].rearrange("p j (c i) -> p c j i", i=4),
            )

        def interleave_w(name, engine, t0, t1):
            copy_on(
                engine,
                grouped[name][:].rearrange("p (t m j) -> p m t j", t=4, j=4)[:, :, t0:t1, :],
                raw[name][:].rearrange("p j (m t) -> p m t j", t=4)[:, :, t0:t1, :],
            )

        def quantize(name, width):
            c = keep.tile([P, width], U32, align_bytes=64, name=f"{name}_codes")
            s = keep.tile([P, width], U8, align_bytes=64, name=f"{name}_scales")
            codes[name] = c
            scales[name] = s
            nc.vector.quantize_mx(out=c[:].bitcast(FP8X4), scales=s[:], in_=grouped[name][:])

        def interleave_e(k, engine):
            g = keep.tile([P, CH * 4], BF16, align_bytes=64, name=f"e{k}_grouped")
            grouped[f"e{k}"] = g
            copy_on(
                engine,
                g[:].rearrange("p (c i j) -> p c j i", i=4, j=4),
                e_raw[k][:].rearrange("p j (c i) -> p c j i", i=4),
            )

        x_grouped = [keep.tile([P, HALF, 4], BF16, align_bytes=64, name=f"x{h}_grouped") for h in range(2)]

        def gather(t, h):
            nc.vector.tensor_copy(
                x_grouped[h][:, :, t], planes[t][:].indirect(offsets[:, h * HALF // 16 : (h + 1) * HALF // 16])
            )

        def quantize_x(h):
            c = keep.tile([P, HALF], U32, align_bytes=64, name=f"x{h}_codes")
            s = keep.tile([P, HALF], U8, align_bytes=64, name=f"x{h}_scales")
            codes[f"x{h}"] = c
            scales[f"x{h}"] = s
            nc.vector.quantize_mx(
                out=c[:].bitcast(FP8X4), scales=s[:], in_=x_grouped[h][:].rearrange("p n j -> p (n j)")
            )

        def product(w, x, c0, acc):
            for t in range(4):
                nc.tensor.matmul_mx(
                    out=acc[:, t, :],
                    lhsT=codes[w][:, t * P : (t + 1) * P].bitcast(FP8X4),
                    lhsT_scale=scales[w][:, t * P : (t + 1) * P],
                    rhs=codes[x][:, c0 : c0 + U].bitcast(FP8X4),
                    rhs_scale=scales[x][:, c0 : c0 + U],
                    start=True,
                    stop=True,
                )

        filt = {}
        cacc = {}
        facc = {}
        oacc = {}
        zc_tiles = {}
        z_tiles = {}

        def f_unit(u):
            acc = psum.tile([P, 4, U], F32, name="f_acc")
            product("w3", f"e{u * U // CH}", u * U % CH, acc)
            facc[u] = acc

        def silu(u):
            s = ring.tile([P, U, 4], F32, name="filter", bufs=8)
            filt[u] = s
            nc.scalar.activation(out=s[:], in_=facc[u][:].rearrange("p t n -> p n t"), func=SILU)

        def c_unit(u):
            acc = psum.tile([P, 4, U], F32, name="c_acc")
            cacc[u] = acc
            product("w1", f"x{u * U // HALF}", u * U % HALF, acc)

        def mult(u, z, col):
            nc.vector.tensor_tensor(
                out=z[:, col * 4 : (col + U) * 4].rearrange("p (n t) -> p n t", t=4),
                in0=cacc[u][:].rearrange("p t n -> p n t"),
                in1=filt[u][:],
                op=MULT,
            )

        def mult_g(u, z, col):
            cs = ring.tile([P, U, 4], F32, name="c_sbuf", bufs=4)
            nc.scalar.copy(out=cs[:], in_=cacc[u][:].rearrange("p t n -> p n t"))
            nc.gpsimd.tensor_tensor(
                out=z[:, col * 4 : (col + U) * 4].rearrange("p (n t) -> p n t", t=4), in0=cs[:], in1=filt[u][:], op=MULT
            )

        def new_z(g):
            n = len(g) * U
            z_tiles[g[0]] = keep.tile([P, n * 4], BF16, align_bytes=64, name=f"z{g[0]}")

        def quantize_z(g):
            n = len(g) * U
            zc = keep.tile([P, n], U32, align_bytes=64, name=f"z{g[0]}_codes")
            zs = keep.tile([P, n], U8, align_bytes=64, name=f"z{g[0]}_scales")
            nc.vector.quantize_mx(out=zc[:].bitcast(FP8X4), scales=zs[:], in_=z_tiles[g[0]][:])
            zc_tiles[g[0]] = (zc, zs)

        def project(g):
            zc, zs = zc_tiles[g[0]]
            acc = psum.tile([P, len(g) * U], F32, name="o_acc", bufs=2)
            oacc[g[0]] = acc
            nc.tensor.matmul_mx(
                out=acc[:],
                lhsT=codes["w2"][:].bitcast(FP8X4),
                lhsT_scale=scales["w2"][:],
                rhs=zc[:].bitcast(FP8X4),
                rhs_scale=zs[:],
                start=True,
                stop=True,
            )

        def store(g, engine):
            n = len(g) * U
            acc = oacc[g[0]]
            y = keep.tile([P, n], F32, name=f"y{g[0]}")
            copy_on(engine, y[:], acc[:])
            nc.sync.dma_start(out=out[:, g[0] * U : g[0] * U + n], in_=y[:])

        gather(0, 0)
        gather(0, 1)
        gather(1, 0)
        gather(1, 1)
        gather(2, 0)
        gather(2, 1)
        gather(3, 0)
        gather(3, 1)
        new_w("w1")
        interleave_w("w1", "G", 2, 4)
        interleave_w("w1", "S", 0, 2)
        quantize_x(0)
        quantize_x(1)
        quantize("w1", 512)
        new_w("w3")
        interleave_w("w3", "S", 0, 2)
        c_unit(0)
        c_unit(1)
        c_unit(2)
        interleave_w("w3", "S", 2, 4)
        interleave_e(0, "V")
        quantize("e0", CH)
        quantize("w3", 512)
        interleave_e(1, "S")
        f_unit(0)
        f_unit(1)
        silu(0)
        quantize("e1", CH)
        interleave_e(2, "V")
        f_unit(2)
        silu(1)
        interleave_w2("G")
        f_unit(3)
        new_z([0, 1])
        mult(0, z_tiles[0], 0 * U)
        silu(2)
        quantize("e2", CH)
        silu(3)
        c_unit(3)
        mult(1, z_tiles[0], 1 * U)
        f_unit(4)
        interleave_e(3, "S")
        f_unit(5)
        quantize("w2", 128)
        quantize_z([0, 1])
        c_unit(4)
        new_z([2, 3])
        mult(2, z_tiles[2], 0 * U)
        project([0, 1])
        silu(4)
        quantize("e3", CH)
        c_unit(5)
        store([0, 1], "S")
        mult(3, z_tiles[2], 1 * U)
        f_unit(6)
        silu(5)
        f_unit(7)
        new_z([4, 5])
        mult(4, z_tiles[4], 0 * U)
        silu(6)
        c_unit(6)
        quantize_z([2, 3])
        c_unit(7)
        silu(7)
        mult(5, z_tiles[4], 1 * U)
        project([2, 3])
        store([2, 3], "S")
        new_z([6])
        mult(6, z_tiles[6], 0 * U)
        quantize_z([4, 5])
        new_z([7])
        mult(7, z_tiles[7], 0 * U)
        project([4, 5])
        store([4, 5], "S")
        quantize_z([6])
        quantize_z([7])
        project([6])
        store([6], "S")
        project([7])
        store([7], "S")
